import numpy as np
import ml_dtypes


def mxq(x, axis, fmt="e4m3"):
    dtype, down = {"e4m3": (ml_dtypes.float8_e4m3fn, 7), "e5m2": (ml_dtypes.float8_e5m2, 14)}[fmt]
    v = np.moveaxis(np.asarray(x, np.float32).astype(ml_dtypes.bfloat16).astype(np.float64), axis, -1)
    blocks = v.reshape(v.shape[:-1] + (-1, 32))
    amax = np.abs(blocks).max(-1, keepdims=True)
    byte = np.maximum(np.where(amax > 0, np.frexp(amax)[1] - 1 + 127, 0) - down, 1)
    scale = np.exp2(byte - 127.0)
    codes = (blocks / scale).astype(np.float32).astype(dtype).astype(np.float64)
    return np.moveaxis((codes * scale).reshape(v.shape), -1, axis)


WIDE = False


def mx_kscale(k):
    if not WIDE:
        return np.ones(k)
    levels = np.array([10, -10, 5, -5, 0])
    if k % 512:
        return np.exp2(np.random.permutation(np.resize(levels, k // 32))).repeat(32)
    a = np.empty((k // 512, 16))
    for p in range(k // 512):
        a[p, :8] = np.random.permutation(np.resize(levels, 8))
        for g in range(8):
            far = levels[np.abs(levels - a[p, g]) >= 10]
            a[p, g + 8] = far[np.random.randint(len(far))]
    return np.exp2(a.ravel()).repeat(32)


def f64(x):
    return np.asarray(x).astype(np.float64)


def striped(idx):
    return np.tile(idx.reshape(-1, 16).T, (8, 1)).astype(np.uint16)


def unstriped(offs):
    return offs[:16].T.reshape(-1).astype(np.int64)


def striped8(idx):
    return np.concatenate([x.reshape(-1, 16).T for x in idx]).astype(np.uint16)


def runs(offs, k):
    lists = np.stack([offs[16 * r : 16 * r + 16].T.reshape(-1) for r in range(8)]).astype(np.int64)
    return lists[np.arange(k) % 512 // 64]


def pack_weight(w):
    k, n = w.shape
    w = f64(np.asarray(w, np.float32).astype(ml_dtypes.bfloat16)).reshape(k // 32, 32, n)
    amax = np.abs(w).max(1)
    byte = np.clip(np.where(amax > 0, np.frexp(amax)[1] - 1 + 127 - 7, 1), 1, 254)
    scaled = (w * np.exp2(127.0 - byte)[:, None, :]).reshape(k, n).astype(np.float32)
    words = np.ascontiguousarray(scaled.reshape(k // 512, 128, 4, n).transpose(0, 1, 3, 2)).astype(ml_dtypes.float8_e4m3fn).view(np.uint8)
    return words, np.ascontiguousarray(byte.astype(np.uint8).reshape(k // 512, 16, n))


def unpack_weight(words, scales):
    g, p, n, _ = words.shape
    vals = np.ascontiguousarray(words).view(ml_dtypes.float8_e4m3fn).astype(np.float64) * np.repeat(np.exp2(scales.astype(np.float64) - 127.0), 8, axis=1)[..., None]
    return vals.transpose(0, 1, 3, 2).reshape(g * 512, n)


def sigmoid(v):
    return 1.0 / (1.0 + np.exp(-np.maximum(v, -700.0)))

def planes(y):
    n, m = y.shape
    v = y.astype(np.float32).astype(ml_dtypes.bfloat16).astype(np.float64).reshape(n // 32, 32, m)
    top = np.abs(v).max(1)
    byte = np.clip(np.where(top > 0, np.frexp(top)[1] - 1 + 127 - 7, 1), 1, 254)
    codes = (v * np.exp2(127.0 - byte)[:, None, :]).reshape(n, m).astype(np.float32).astype(ml_dtypes.float8_e4m3fn).view(np.uint8)
    words = codes.reshape(n // 512, 128, 4, m).transpose(0, 1, 3, 2)
    return np.ascontiguousarray(words), np.ascontiguousarray(byte.astype(np.uint8).reshape(n // 512, 16, m))


K, T, S, G, H, W = 512, 1024, 512, 2048, 512, 256


def setup_inputs():
    n = np.random.standard_normal
    s = mx_kscale(K)[:, None]
    packed_xT = pack_weight(n((K, T)) * s)
    packed_dT = pack_weight(n((K, G)) / s)
    perm = np.stack([np.random.permutation(S) for _ in range(8)])
    return {
        "x_words": packed_xT[0],
        "x_scales": packed_xT[1],
        "d_words": packed_dT[0],
        "d_scales": packed_dT[1],
        "gs": (np.random.uniform(0.5, 1.5, (K, 1)) * s).astype(np.float32),
        "offs": striped(np.random.permutation(T)[:S]),
        "k1": striped8(np.random.randint(0, G, (8, H))),
        "n1": striped8(np.stack([np.random.permutation(S) for _ in range(8)])),
        "n2": striped8(np.stack([np.random.permutation(S) for _ in range(8)])),
        "k2": striped8(np.random.randint(0, G, (8, H))),
        "n3": striped8(perm[:, :W]),
        "n4": striped8(perm[:, W:]),
    }


def reference(x_words, x_scales, d_words, d_scales, gs, offs, k1, n1, n2, k2, n3, n4):
    d_k2 = unpack_weight(d_words, d_scales)[np.arange(K)[:, None], runs(k2, K)]
    d_k1 = unpack_weight(d_words, d_scales)[np.arange(K)[:, None], runs(k1, K)]
    xq = unpack_weight(x_words, x_scales)[:, unstriped(offs)]
    h = 0.0625 * (d_k1.T @ xq)
    st = h - (h[np.arange(H)[:, None], runs(n1, H)])
    z = f64(gs) * (st / (np.abs(st[np.arange(H)[:, None], runs(n2, H)]) + 0.5))
    h2 = 0.0625 * ((d_k2.T @ mxq(z, 0, "e4m3")))
    pb = h2[np.arange(H)[:, None], runs(n4, H)]
    pa = h2[np.arange(H)[:, None], runs(n3, H)]
    rb = pb * sigmoid(pb - pa)
    ra = pa * sigmoid(pa - pb)
    ds = np.zeros((H, S))
    ds[np.arange(H)[:, None], runs(n3, H)] = ra
    out = ds.copy()
    out[np.arange(H)[:, None], runs(n4, H)] = rb
    return (out,) + planes(out)

@@ -1,0 +1,257 @@
+from contextlib import ExitStack
+
+import concourse.mybir as mybir
+
+K, T, S, G, H, W = 512, 1024, 512, 2048, 512, 256
+FLOPS = 2 * (2 * K * H * S)
+
+F32 = mybir.dt.float32
+BF16 = mybir.dt.bfloat16
+I32 = mybir.dt.int32
+U32 = mybir.dt.uint32
+U16 = mybir.dt.uint16
+U8 = mybir.dt.uint8
+FP8X4 = mybir.dt.float8_e4m3fn_x4
+ACT = mybir.ActivationFunctionType
+ALU = mybir.AluOpType
+
+P = 128
+PACK = 4
+HALF = S // 2
+TINY = 2.0 ** -100
+
+
+def tile_picked_codehopnduel_none_po_kernel(
+    tc, x_words, x_scales, d_words, d_scales, gs, offs, k1, n1, n2, k2, n3, n4, out_0, out_1, out_2
+):
+    nc = tc.nc
+    with ExitStack() as ctx:
+        lists = ctx.enter_context(tc.tile_pool(name="lists", bufs=1))
+        keep = ctx.enter_context(tc.tile_pool(name="keep", bufs=1))
+        psum = ctx.enter_context(tc.psum_pool(name="psum", bufs=1))
+
+        def list_tile(name, entries):
+            return lists.tile([P, entries // 16], U16, name=name)
+
+        k1_t, offs_t = list_tile("k1_t", H), list_tile("offs_t", S)
+        n1_t, k2_t, n2_t = list_tile("n1_t", S), list_tile("k2_t", H), list_tile("n2_t", S)
+        n3_t, n4_t = list_tile("n3_t", W), list_tile("n4_t", W)
+
+        def sb(name, shape, dtype, tag=""):
+            return keep.tile(shape, dtype, name=name, tag=tag, align_bytes=64)
+
+        d_bytes = sb("d_bytes", [P, G], U8)
+        x_bytes = sb("x_bytes", [P, T], U8)
+        d_codes = sb("d_codes", [P, G], I32)
+        x_codes = sb("x_codes", [P, T], I32)
+        gs_t = sb("gs_t", [P, PACK], F32)
+        w_plane = [sb("w_plane%d" % i, [P, H], U8) for i in range(2)]
+        h_win = [sb("h_win%d" % t, [P, 2 * S], F32, tag="h_win%d" % t) for t in range(PACK)]
+        h_last = sb("h_last", [P, S], F32)
+        h_own = [h_win[t + 1][:, S:] for t in range(PACK - 1)] + [h_last[:]]
+
+        nc.sync.dma_start(k1_t[:], k1)
+        nc.sync.dma_start(d_bytes[:].bitcast(I32), d_scales[0].bitcast(I32).unsqueeze(1).to_broadcast([16, 8, G // 4]))
+        nc.sync.dma_start(offs_t[:], offs)
+        nc.sync.dma_start(x_codes[:], x_words[0].rearrange("p n t -> p (n t)").bitcast(I32))
+        nc.sync.dma_start(d_codes[:], d_words[0].rearrange("p n t -> p (n t)").bitcast(I32))
+        for q in range(4):
+            nc.scalar.dma_start(
+                x_bytes[32 * q : 32 * q + 32, :].bitcast(I32),
+                x_scales[0, 4 * q : 4 * q + 4, :].bitcast(I32).unsqueeze(0).to_broadcast([8, 4, T // 4]),
+            )
+        nc.scalar.dma_start(gs_t[:], gs.rearrange("(p t) o -> p (t o)", t=PACK))
+        for tile, src in ((k2_t, k2), (n1_t, n1), (n2_t, n2), (n3_t, n3), (n4_t, n4)):
+            nc.sync.dma_start(tile[:], src)
+        for plane in w_plane:
+            nc.gpsimd.memset(plane[:].bitcast(I32), 0)
+        nc.gpsimd.memset(h_win[0][:, S:], 0.0)
+
+        inv_root = sb("inv_root", [P, PACK], F32)
+        size = sb("size", [P, PACK], F32)
+        sign = sb("sign", [P, PACK], F32)
+        h_scale = sb("h_scale", [P, PACK], F32)
+        guess = sb("guess", [P, PACK], F32)
+        miss = sb("miss", [P, PACK], F32)
+        mend = sb("mend", [P, PACK], F32)
+        root = sb("root", [P, PACK], F32)
+        nc.scalar.activation(inv_root[:], gs_t[:], ACT.Abs_reciprocal_sqrt, bias=TINY)
+        nc.scalar.activation(size[:], gs_t[:], ACT.Abs)
+        nc.scalar.activation(sign[:], gs_t[:], ACT.Sign)
+        nc.scalar.activation(h_scale[:], sign[:], ACT.Copy, scale=-0.0625)
+        nc.gpsimd.tensor_tensor(guess[:], size[:], inv_root[:], ALU.mult)
+        nc.gpsimd.tensor_tensor(miss[:], guess[:], inv_root[:], ALU.mult)
+        nc.gpsimd.tensor_scalar(mend[:], miss[:], -0.5, 1.5, ALU.mult, ALU.add)
+        nc.gpsimd.tensor_tensor(root[:], guess[:], mend[:], ALU.mult)
+
+        def pick_scales(i, codes, tag):
+            picked = sb("picked_bytes%d" % i, [P, H], U8, tag=tag)
+            dealt = sb("dealt_bytes%d" % i, [P, H], U8)
+            nc.vector.tensor_copy(picked[:], d_bytes[:].indirect(codes[:]))
+            nc.vector.tensor_copy(
+                dealt[:].rearrange("p (t m) -> p t m", t=PACK), picked[:].rearrange("p (m t) -> p t m", t=PACK)
+            )
+            for q in range(4):
+                nc.sync.dma_start(
+                    w_plane[i][32 * q : 32 * q + 4, :].bitcast(I32), dealt[32 * q : 32 * q + 32 : 8, :].bitcast(I32)
+                )
+
+        def pick_words(i, codes, tag):
+            picked = sb("picked_words%d" % i, [P, H], U32, tag=tag)
+            dealt = sb("dealt_words%d" % i, [P, H], U32)
+            nc.vector.tensor_copy(picked[:], d_codes[:].bitcast(U32).indirect(codes[:]))
+            nc.vector.tensor_copy(
+                dealt[:].rearrange("p (t m) -> p t m", t=PACK).bitcast(I32),
+                picked[:].bitcast(I32).rearrange("p (m t) -> p t m", t=PACK),
+            )
+            return dealt
+
+        pick_scales(0, k1_t, "")
+        xq_words = sb("xq_words", [P, S], U32)
+        xq_plane = sb("xq_plane", [P, S], U8)
+        nc.vector.tensor_copy(xq_words[:], x_codes[:].bitcast(U32).indirect(offs_t[:]))
+        nc.vector.tensor_copy(xq_plane[:], x_bytes[:].indirect(offs_t[:]))
+        w1 = pick_words(0, k1_t, "first_words")
+
+        def product(out, i, words, t, rhs_words, rhs_plane, cols):
+            rows = slice(P * t, P * (t + 1))
+            nc.tensor.matmul_mx(
+                out=out,
+                lhsT=words[:, rows].bitcast(FP8X4),
+                lhsT_scale=w_plane[i][:, rows],
+                rhs=rhs_words[:, cols].bitcast(FP8X4),
+                rhs_scale=rhs_plane[:, cols],
+                start=True,
+                stop=True,
+            )
+
+        h_bank = [psum.tile([P, S], F32, name="h_bank%d" % t, tag="bank%d" % t) for t in range(PACK)]
+        for t in range(PACK):
+            product(h_bank[t][:], 0, w1, t, xq_words, xq_plane, slice(0, S))
+
+        pick_scales(1, k2_t, "first_words")
+
+        st = sb("st", [P, PACK, S], F32)
+        mag = sb("mag", [P, PACK, S], F32)
+        gain = [sb("gain%d" % t, [P, 2 * S], F32) for t in range(PACK)]
+        z = sb("z", [P, PACK, S], F32)
+
+        def step(t):
+            nc.scalar.activation(h_win[t][:, :S], h_bank[t][:], ACT.Copy, scale=h_scale[:, t : t + 1])
+            nc.scalar.activation(h_own[t], h_bank[t][:], ACT.Copy, scale=h_scale[:, t : t + 1])
+            nc.vector.tensor_tensor(st[:, t, :], h_win[t][:].indirect(n1_t[:]), h_own[t], ALU.subtract)
+
+        def weigh(t):
+            nc.scalar.activation(mag[:, t, :], st[:, t, :], ACT.Abs)
+            nc.scalar.activation(gain[t][:, S:], mag[:, t, :], ACT.Abs_reciprocal_sqrt, bias=0.5)
+            nc.scalar.activation(gain[t][:, :S], gain[t][:, S:], ACT.Square, scale=root[:, t : t + 1])
+
+        def divide(t, a, b):
+            places = n2_t[:, a // 16 : b // 16]
+            nc.vector.tensor_tensor(z[:, t, a:b], gain[t][:].indirect(places), st[:, t, a:b], ALU.mult)
+
+        z_packed = sb("z_packed", [P, S * PACK], BF16)
+        z_words = sb("z_words", [P, S], U32)
+        z_plane = sb("z_plane", [P, S], U8)
+
+        def weave(copy, a, b):
+            copy(
+                z_packed[:, PACK * a : PACK * b].rearrange("p (c i t) -> p c t i", i=4, t=PACK),
+                z[:, :, a:b].rearrange("p t (c i) -> p c t i", i=4),
+            )
+
+        step(0)
+        step(1)
+        w2 = pick_words(1, k2_t, "h_win0")
+        weigh(0)
+        step(2)
+        divide(0, 0, S)
+        weigh(1)
+        step(3)
+        divide(1, 0, S)
+        weigh(2)
+        divide(2, 0, S)
+        weigh(3)
+        quarter = S // 4
+        for a in (0, quarter):
+            divide(3, a, a + quarter)
+            weave(nc.scalar.copy, a, a + quarter)
+        divide(3, HALF, S)
+        weave(nc.vector.tensor_copy, HALF, S)
+
+        h2_bank = [
+            [psum.tile([P, HALF], F32, name="h2_bank%d_%d" % (u, t), tag="bank%d" % (PACK * (1 - u) + t)) for t in range(PACK)]
+            for u in range(2)
+        ]
+        halves = [slice(HALF * u, HALF * (u + 1)) for u in range(2)]
+        for u in range(2):
+            wide = slice(PACK * HALF * u, PACK * HALF * (u + 1))
+            nc.vector.quantize_mx(
+                out=z_words[:, halves[u]].bitcast(FP8X4), scales=z_plane[:, halves[u]], in_=z_packed[:, wide]
+            )
+        for t in range(PACK):
+            for u in range(2):
+                product(h2_bank[u][t][:], 1, w2, t, z_words, z_plane, halves[u])
+
+        res = [sb("res%d" % t, [P, S], F32) for t in range(PACK)]
+        pa = sb("pa", [P, PACK, W], F32)
+        pb = sb("pb", [P, PACK, W], F32)
+        sa = sb("sa", [P, PACK, W], F32)
+        sbb = sb("sbb", [P, PACK, W], F32)
+        y_packed = sb("y_packed", [P, S, PACK], BF16)
+        y_words = sb("y_words", [P, S], U32)
+        y_plane = sb("y_plane", [P, S], U8)
+        out_rows = out_0.rearrange("(p t) s -> t p s", t=PACK)
+
+        def fetch(t):
+            h2 = sb("h2_%d" % t, [P, S], F32)
+            for u in range(2):
+                nc.scalar.activation(h2[:, halves[u]], h2_bank[u][t][:], ACT.Copy, scale=0.0625)
+            nc.vector.tensor_copy(pa[:, t, :], h2[:].indirect(n3_t[:]))
+            nc.vector.tensor_copy(pb[:, t, :], h2[:].indirect(n4_t[:]))
+
+        def gates(t):
+            gap = sb("gap%d" % t, [P, W], F32)
+            nc.vector.tensor_tensor(gap[:], pb[:, t, :], pa[:, t, :], ALU.subtract)
+            nc.scalar.activation(sa[:, t, :], gap[:], ACT.Sigmoid, scale=-1.0)
+            nc.scalar.activation(sbb[:, t, :], gap[:], ACT.Sigmoid)
+
+        def put_a(t):
+            nc.vector.tensor_tensor(res[t][:].indirect(n3_t[:]), pa[:, t, :], sa[:, t, :], ALU.mult)
+
+        def put_b(t):
+            nc.vector.tensor_tensor(res[t][:].indirect(n4_t[:]), pb[:, t, :], sbb[:, t, :], ALU.mult)
+            nc.sync.dma_start(out_rows[t], res[t][:])
+
+        split = 3 * quarter
+        fetch(0)
+        for t in range(1, PACK):
+            fetch(t)
+            gates(t - 1)
+        gates(PACK - 1)
+        put_a(0)
+        for t in range(2):
+            put_a(t + 1)
+            put_b(t)
+            nc.scalar.copy(y_packed[:, :, t], res[t][:])
+        put_a(3)
+        put_b(2)
+        nc.scalar.copy(y_packed[:, :split, 2:], res[2][:, :split].unsqueeze(2).to_broadcast([P, split, 2]))
+        nc.scalar.copy(y_packed[:, split:, 2], res[2][:, split:])
+        put_b(3)
+        nc.scalar.copy(y_packed[:, split:, 3], res[3][:, split:])
+        nc.vector.tensor_copy(y_packed[:, :HALF, 3], res[3][:, :HALF])
+        nc.vector.tensor_copy(y_packed[:, HALF:split, 3], res[3][:, HALF:split])
+
+        words_out = out_1[0].rearrange("p n t -> p (n t)").bitcast(I32)
+        for u in range(2):
+            nc.vector.quantize_mx(
+                out=y_words[:, halves[u]].bitcast(FP8X4),
+                scales=y_plane[:, halves[u]],
+                in_=y_packed[:, halves[u], :].rearrange("p s t -> p (s t)"),
+            )
+            nc.sync.dma_start(words_out[:, halves[u]], y_words[:, halves[u]].bitcast(I32))
+        for q in range(4):
+            nc.scalar.dma_start(
+                out_2[0, 4 * q : 4 * q + 4, :].bitcast(I32), y_plane[32 * q : 32 * q + 4, :].bitcast(I32)
+            )

@@ -1,6 +1,7 @@
 from contextlib import ExitStack
 
 import concourse.mybir as mybir
+from concourse.masks import make_identity
 
 K, T, S, G, H, W = 512, 1024, 512, 2048, 512, 256
 FLOPS = 2 * (2 * K * H * S)
@@ -46,26 +47,28 @@ def tile_picked_codehopnduel_none_po_kernel(
         x_codes = sb("x_codes", [P, T], I32)
         gs_t = sb("gs_t", [P, PACK], F32)
         w_plane = [sb("w_plane%d" % i, [P, H], U8) for i in range(2)]
-        h_win = [sb("h_win%d" % t, [P, 2 * S], F32, tag="h_win%d" % t) for t in range(PACK)]
+        h_win = [sb("h_win%d" % t, [P, 2 * S], F32) for t in range(PACK)]
         h_last = sb("h_last", [P, S], F32)
         h_own = [h_win[t + 1][:, S:] for t in range(PACK - 1)] + [h_last[:]]
 
         nc.sync.dma_start(k1_t[:], k1)
         nc.sync.dma_start(d_bytes[:].bitcast(I32), d_scales[0].bitcast(I32).unsqueeze(1).to_broadcast([16, 8, G // 4]))
         nc.sync.dma_start(offs_t[:], offs)
-        nc.sync.dma_start(x_codes[:], x_words[0].rearrange("p n t -> p (n t)").bitcast(I32))
-        nc.sync.dma_start(d_codes[:], d_words[0].rearrange("p n t -> p (n t)").bitcast(I32))
         for q in range(4):
             nc.scalar.dma_start(
                 x_bytes[32 * q : 32 * q + 32, :].bitcast(I32),
                 x_scales[0, 4 * q : 4 * q + 4, :].bitcast(I32).unsqueeze(0).to_broadcast([8, 4, T // 4]),
             )
+        nc.sync.dma_start(x_codes[:], x_words[0].rearrange("p n t -> p (n t)").bitcast(I32))
+        nc.sync.dma_start(d_codes[:], d_words[0].rearrange("p n t -> p (n t)").bitcast(I32))
         nc.scalar.dma_start(gs_t[:], gs.rearrange("(p t) o -> p (t o)", t=PACK))
         for tile, src in ((k2_t, k2), (n1_t, n1), (n2_t, n2), (n3_t, n3), (n4_t, n4)):
             nc.sync.dma_start(tile[:], src)
         for plane in w_plane:
             nc.gpsimd.memset(plane[:].bitcast(I32), 0)
         nc.gpsimd.memset(h_win[0][:, S:], 0.0)
+        ident = sb("ident", [P, P], F32)
+        make_identity(nc, ident[:])
 
         inv_root = sb("inv_root", [P, PACK], F32)
         size = sb("size", [P, PACK], F32)
@@ -86,32 +89,44 @@ def tile_picked_codehopnduel_none_po_kernel(
 
         def pick_scales(i, codes, tag):
             picked = sb("picked_bytes%d" % i, [P, H], U8, tag=tag)
-            dealt = sb("dealt_bytes%d" % i, [P, H], U8)
             nc.vector.tensor_copy(picked[:], d_bytes[:].indirect(codes[:]))
+            return picked
+
+        def deal_scales(i, picked, queue):
+            dealt = sb("dealt_bytes%d" % i, [P, H], U8)
             nc.vector.tensor_copy(
-                dealt[:].rearrange("p (t m) -> p t m", t=PACK), picked[:].rearrange("p (m t) -> p t m", t=PACK)
+                dealt[:].rearrange("p (t m) -> p m t", t=PACK), picked[:].rearrange("p (m t) -> p m t", t=PACK)
             )
             for q in range(4):
-                nc.sync.dma_start(
+                queue.dma_start(
                     w_plane[i][32 * q : 32 * q + 4, :].bitcast(I32), dealt[32 * q : 32 * q + 32 : 8, :].bitcast(I32)
                 )
 
-        def pick_words(i, codes, tag):
-            picked = sb("picked_words%d" % i, [P, H], U32, tag=tag)
-            dealt = sb("dealt_words%d" % i, [P, H], U32)
-            nc.vector.tensor_copy(picked[:], d_codes[:].bitcast(U32).indirect(codes[:]))
-            nc.vector.tensor_copy(
-                dealt[:].rearrange("p (t m) -> p t m", t=PACK).bitcast(I32),
-                picked[:].bitcast(I32).rearrange("p (m t) -> p t m", t=PACK),
-            )
-            return dealt
+        def pick_words(name, codes, tag):
+            picked = sb(name, [P, 16 * codes.shape[1]], U32, tag=tag)
+            nc.vector.tensor_copy(picked[:], d_codes[:].bitcast(U32).indirect(codes))
+            return picked
 
-        pick_scales(0, k1_t, "")
+        def deal_words(dealt, picked, m0):
+            m1 = m0 + picked.shape[1] // PACK
+            nc.vector.tensor_copy(
+                dealt[:].bitcast(I32).rearrange("p (t m) -> p m t", t=PACK)[:, m0:m1, :],
+                picked[:].bitcast(I32).rearrange("p (m t) -> p m t", t=PACK),
+            )
+
+        w1 = sb("w1", [P, H], U32)
+        w2 = sb("w2", [P, H], U32)
         xq_words = sb("xq_words", [P, S], U32)
         xq_plane = sb("xq_plane", [P, S], U8)
-        nc.vector.tensor_copy(xq_words[:], x_codes[:].bitcast(U32).indirect(offs_t[:]))
+        bytes1 = pick_scales(0, k1_t, "")
         nc.vector.tensor_copy(xq_plane[:], x_bytes[:].indirect(offs_t[:]))
-        w1 = pick_words(0, k1_t, "first_words")
+        deal_scales(0, bytes1, nc.scalar)
+        nc.vector.tensor_copy(xq_words[:], x_codes[:].bitcast(U32).indirect(offs_t[:]))
+        words1 = [pick_words("words1_%d" % u, k1_t[:, 16 * u : 16 * (u + 1)], "early%d" % u) for u in range(2)]
+        for u in range(2):
+            deal_words(w1, words1[u], P // 2 * u)
+        bytes2 = pick_scales(1, k2_t, "early0")
+        words2 = pick_words("words2", k2_t[:], "early1")
 
         def product(out, i, words, t, rhs_words, rhs_plane, cols):
             rows = slice(P * t, P * (t + 1))
@@ -126,25 +141,37 @@ def tile_picked_codehopnduel_none_po_kernel(
             )
 
         h_bank = [psum.tile([P, S], F32, name="h_bank%d" % t, tag="bank%d" % t) for t in range(PACK)]
-        for t in range(PACK):
+        for t in (0, 2, 1, 3):
             product(h_bank[t][:], 0, w1, t, xq_words, xq_plane, slice(0, S))
 
-        pick_scales(1, k2_t, "first_words")
+        deal_scales(1, bytes2, nc.sync)
 
         st = sb("st", [P, PACK, S], F32)
         mag = sb("mag", [P, PACK, S], F32)
         gain = [sb("gain%d" % t, [P, 2 * S], F32) for t in range(PACK)]
         z = sb("z", [P, PACK, S], F32)
 
-        def step(t):
+        def spill(t):
             nc.scalar.activation(h_win[t][:, :S], h_bank[t][:], ACT.Copy, scale=h_scale[:, t : t + 1])
-            nc.scalar.activation(h_own[t], h_bank[t][:], ACT.Copy, scale=h_scale[:, t : t + 1])
+            if t < 2:
+                nc.scalar.activation(h_own[t], h_bank[t][:], ACT.Copy, scale=h_scale[:, t : t + 1])
+            else:
+                nc.sync.dma_start(h_own[t], h_win[t][:, :S])
+
+        def step(t):
             nc.vector.tensor_tensor(st[:, t, :], h_win[t][:].indirect(n1_t[:]), h_own[t], ALU.subtract)
 
         def weigh(t):
-            nc.scalar.activation(mag[:, t, :], st[:, t, :], ACT.Abs)
-            nc.scalar.activation(gain[t][:, S:], mag[:, t, :], ACT.Abs_reciprocal_sqrt, bias=0.5)
-            nc.scalar.activation(gain[t][:, :S], gain[t][:, S:], ACT.Square, scale=root[:, t : t + 1])
+            for a in (0, HALF):
+                nc.scalar.activation(mag[:, t, a : a + HALF], st[:, t, a : a + HALF], ACT.Abs)
+            for a in (0, HALF):
+                nc.scalar.activation(
+                    gain[t][:, S + a : S + a + HALF], mag[:, t, a : a + HALF], ACT.Abs_reciprocal_sqrt, bias=0.5
+                )
+            for a in (0, HALF):
+                nc.scalar.activation(
+                    gain[t][:, a : a + HALF], gain[t][:, S + a : S + a + HALF], ACT.Square, scale=root[:, t : t + 1]
+                )
 
         def divide(t, a, b):
             places = n2_t[:, a // 16 : b // 16]
@@ -160,24 +187,21 @@ def tile_picked_codehopnduel_none_po_kernel(
                 z[:, :, a:b].rearrange("p t (c i) -> p c t i", i=4),
             )
 
+        for t in (0, 2, 1, 3):
+            spill(t)
         step(0)
+        deal_words(w2, words2, 0)
         step(1)
-        w2 = pick_words(1, k2_t, "h_win0")
-        weigh(0)
-        step(2)
-        divide(0, 0, S)
-        weigh(1)
-        step(3)
-        divide(1, 0, S)
-        weigh(2)
-        divide(2, 0, S)
-        weigh(3)
+        for t in range(2, PACK):
+            step(t)
+        for t in range(PACK):
+            weigh(t)
+        for t in range(PACK - 1):
+            divide(t, 0, S)
         quarter = S // 4
-        for a in (0, quarter):
+        for a in range(0, S, quarter):
             divide(3, a, a + quarter)
-            weave(nc.scalar.copy, a, a + quarter)
-        divide(3, HALF, S)
-        weave(nc.vector.tensor_copy, HALF, S)
+            weave(nc.vector.tensor_copy if a + quarter == S else nc.scalar.copy, a, a + quarter)
 
         h2_bank = [
             [psum.tile([P, HALF], F32, name="h2_bank%d_%d" % (u, t), tag="bank%d" % (PACK * (1 - u) + t)) for t in range(PACK)]
@@ -203,18 +227,34 @@ def tile_picked_codehopnduel_none_po_kernel(
         y_plane = sb("y_plane", [P, S], U8)
         out_rows = out_0.rearrange("(p t) s -> t p s", t=PACK)
 
-        def fetch(t):
-            h2 = sb("h2_%d" % t, [P, S], F32)
-            for u in range(2):
-                nc.scalar.activation(h2[:, halves[u]], h2_bank[u][t][:], ACT.Copy, scale=0.0625)
-            nc.vector.tensor_copy(pa[:, t, :], h2[:].indirect(n3_t[:]))
-            nc.vector.tensor_copy(pb[:, t, :], h2[:].indirect(n4_t[:]))
+        h2 = [sb("h2_%d" % t, [P, S], F32) for t in range(PACK)]
+        gap = sb("gap", [P, PACK, W], F32)
+        turned = sb("turned", [P, PACK, W], F32)
 
-        def gates(t):
-            gap = sb("gap%d" % t, [P, W], F32)
-            nc.vector.tensor_tensor(gap[:], pb[:, t, :], pa[:, t, :], ALU.subtract)
-            nc.scalar.activation(sa[:, t, :], gap[:], ACT.Sigmoid, scale=-1.0)
-            nc.scalar.activation(sbb[:, t, :], gap[:], ACT.Sigmoid)
+        def fetch(t):
+            for u in range(2):
+                nc.scalar.activation(h2[t][:, halves[u]], h2_bank[u][t][:], ACT.Copy, scale=0.0625)
+            nc.vector.tensor_copy(pa[:, t, :], h2[t][:].indirect(n3_t[:]))
+
+        def face(t):
+            nc.vector.tensor_tensor(gap[:, t, :], h2[t][:].indirect(n4_t[:]), pa[:, t, :], ALU.subtract)
+
+        def gate_a(t):
+            nc.scalar.activation(sa[:, t, :], gap[:, t, :], ACT.Sigmoid, scale=-1.0)
+
+        def gate_b(t):
+            there = psum.tile([P, W], F32, name="there%d" % t, tag="bank%d" % t)
+            back = psum.tile([P, W], F32, name="back%d" % t, tag="bank%d" % (PACK + t))
+            for c in range(0, W, P):
+                for first, part in ((True, pa), (False, gap)):
+                    nc.tensor.matmul(
+                        there[:, c : c + P], part[:, t, c : c + P], ident[:], start=first, stop=not first, is_transpose=True
+                    )
+            nc.scalar.copy(turned[:, t, :], there[:])
+            for c in range(0, W, P):
+                nc.tensor.transpose(back[:, c : c + P], turned[:, t, c : c + P], ident[:])
+            nc.scalar.activation(sbb[:, t, :], gap[:, t, :], ACT.Sigmoid)
+            nc.scalar.copy(pb[:, t, :], back[:])
 
         def put_a(t):
             nc.vector.tensor_tensor(res[t][:].indirect(n3_t[:]), pa[:, t, :], sa[:, t, :], ALU.mult)
@@ -227,8 +267,13 @@ def tile_picked_codehopnduel_none_po_kernel(
         fetch(0)
         for t in range(1, PACK):
             fetch(t)
-            gates(t - 1)
-        gates(PACK - 1)
+            face(t - 1)
+        face(PACK - 1)
+        gate_a(0)
+        for t in range(1, PACK):
+            gate_a(t)
+            gate_b(t - 1)
+        gate_b(PACK - 1)
         put_a(0)
         for t in range(2):
             put_a(t + 1)

@@ -65,27 +65,29 @@ def tile_picked_codehopnduel_none_po_kernel(
         for tile, src in ((k2_t, k2), (n1_t, n1), (n2_t, n2), (n3_t, n3), (n4_t, n4)):
             nc.sync.dma_start(tile[:], src)
         for plane in w_plane:
-            nc.gpsimd.memset(plane[:].bitcast(I32), 0)
-        nc.gpsimd.memset(h_win[0][:, S:], 0.0)
+            nc.vector.memset(plane[:].bitcast(I32), 0)
+        nc.vector.memset(h_win[0][:, S:], 0.0)
         ident = sb("ident", [P, P], F32)
         make_identity(nc, ident[:])
 
         inv_root = sb("inv_root", [P, PACK], F32)
-        size = sb("size", [P, PACK], F32)
+        half_inv = sb("half_inv", [P, PACK], F32)
         sign = sb("sign", [P, PACK], F32)
         h_scale = sb("h_scale", [P, PACK], F32)
         guess = sb("guess", [P, PACK], F32)
-        miss = sb("miss", [P, PACK], F32)
         mend = sb("mend", [P, PACK], F32)
         root = sb("root", [P, PACK], F32)
+        cells = [slice(t, t + 1) for t in range(PACK)]
         nc.scalar.activation(inv_root[:], gs_t[:], ACT.Abs_reciprocal_sqrt, bias=TINY)
-        nc.scalar.activation(size[:], gs_t[:], ACT.Abs)
         nc.scalar.activation(sign[:], gs_t[:], ACT.Sign)
+        nc.scalar.activation(half_inv[:], inv_root[:], ACT.Copy, scale=-0.5)
         nc.scalar.activation(h_scale[:], sign[:], ACT.Copy, scale=-0.0625)
-        nc.gpsimd.tensor_tensor(guess[:], size[:], inv_root[:], ALU.mult)
-        nc.gpsimd.tensor_tensor(miss[:], guess[:], inv_root[:], ALU.mult)
-        nc.gpsimd.tensor_scalar(mend[:], miss[:], -0.5, 1.5, ALU.mult, ALU.add)
-        nc.gpsimd.tensor_tensor(root[:], guess[:], mend[:], ALU.mult)
+        for c in cells:
+            nc.scalar.activation(guess[:, c], gs_t[:, c], ACT.Abs, scale=inv_root[:, c])
+        for c in cells:
+            nc.scalar.activation(mend[:, c], guess[:, c], ACT.Identity, scale=half_inv[:, c], bias=1.5)
+        for c in cells:
+            nc.scalar.activation(root[:, c], guess[:, c], ACT.Copy, scale=mend[:, c])
 
         def pick_scales(i, codes, tag):
             picked = sb("picked_bytes%d" % i, [P, H], U8, tag=tag)
@@ -297,6 +299,6 @@ def tile_picked_codehopnduel_none_po_kernel(
             )
             nc.sync.dma_start(words_out[:, halves[u]], y_words[:, halves[u]].bitcast(I32))
         for q in range(4):
-            nc.scalar.dma_start(
+            (nc.scalar if q < 2 else nc.sync).dma_start(
                 out_2[0, 4 * q : 4 * q + 4, :].bitcast(I32), y_plane[32 * q : 32 * q + 4, :].bitcast(I32)
             )

from contextlib import ExitStack

import concourse.mybir as mybir
from concourse.masks import make_identity

K, T, S, G, H, W = 512, 1024, 512, 2048, 512, 256
FLOPS = 2 * (2 * K * H * S)

F32 = mybir.dt.float32
BF16 = mybir.dt.bfloat16
I32 = mybir.dt.int32
U32 = mybir.dt.uint32
U16 = mybir.dt.uint16
U8 = mybir.dt.uint8
FP8X4 = mybir.dt.float8_e4m3fn_x4
ACT = mybir.ActivationFunctionType
ALU = mybir.AluOpType

P = 128
PACK = 4
HALF = S // 2
TINY = 2.0 ** -100


def tile_picked_codehopnduel_none_po_kernel(
    tc, x_words, x_scales, d_words, d_scales, gs, offs, k1, n1, n2, k2, n3, n4, out_0, out_1, out_2
):
    nc = tc.nc
    with ExitStack() as ctx:
        lists = ctx.enter_context(tc.tile_pool(name="lists", bufs=1))
        keep = ctx.enter_context(tc.tile_pool(name="keep", bufs=1))
        psum = ctx.enter_context(tc.psum_pool(name="psum", bufs=1))

        def list_tile(name, entries):
            return lists.tile([P, entries // 16], U16, name=name)

        k1_t, offs_t = list_tile("k1_t", H), list_tile("offs_t", S)
        n1_t, k2_t, n2_t = list_tile("n1_t", S), list_tile("k2_t", H), list_tile("n2_t", S)
        n3_t, n4_t = list_tile("n3_t", W), list_tile("n4_t", W)

        def sb(name, shape, dtype, tag=""):
            return keep.tile(shape, dtype, name=name, tag=tag, align_bytes=64)

        d_bytes = sb("d_bytes", [P, G], U8)
        x_bytes = sb("x_bytes", [P, T], U8)
        d_codes = sb("d_codes", [P, G], I32)
        x_codes = sb("x_codes", [P, T], I32)
        gs_t = sb("gs_t", [P, PACK], F32)
        w_plane = [sb("w_plane%d" % i, [P, H], U8) for i in range(2)]
        h_win = [sb("h_win%d" % t, [P, 2 * S], F32) for t in range(PACK)]
        h_last = sb("h_last", [P, S], F32)
        h_own = [h_win[t + 1][:, S:] for t in range(PACK - 1)] + [h_last[:]]

        nc.sync.dma_start(k1_t[:], k1)
        nc.sync.dma_start(d_bytes[:].bitcast(I32), d_scales[0].bitcast(I32).unsqueeze(1).to_broadcast([16, 8, G // 4]))
        nc.sync.dma_start(offs_t[:], offs)
        for q in range(4):
            nc.scalar.dma_start(
                x_bytes[32 * q : 32 * q + 32, :].bitcast(I32),
                x_scales[0, 4 * q : 4 * q + 4, :].bitcast(I32).unsqueeze(0).to_broadcast([8, 4, T // 4]),
            )
        nc.sync.dma_start(x_codes[:], x_words[0].rearrange("p n t -> p (n t)").bitcast(I32))
        nc.sync.dma_start(d_codes[:], d_words[0].rearrange("p n t -> p (n t)").bitcast(I32))
        nc.scalar.dma_start(gs_t[:], gs.rearrange("(p t) o -> p (t o)", t=PACK))
        for tile, src in ((k2_t, k2), (n1_t, n1), (n2_t, n2), (n3_t, n3), (n4_t, n4)):
            nc.sync.dma_start(tile[:], src)
        for plane in w_plane:
            nc.vector.memset(plane[:].bitcast(I32), 0)
        nc.vector.memset(h_win[0][:, S:], 0.0)
        ident = sb("ident", [P, P], F32)
        make_identity(nc, ident[:])

        inv_root = sb("inv_root", [P, PACK], F32)
        half_inv = sb("half_inv", [P, PACK], F32)
        sign = sb("sign", [P, PACK], F32)
        h_scale = sb("h_scale", [P, PACK], F32)
        guess = sb("guess", [P, PACK], F32)
        mend = sb("mend", [P, PACK], F32)
        root = sb("root", [P, PACK], F32)
        cells = [slice(t, t + 1) for t in range(PACK)]
        nc.scalar.activation(inv_root[:], gs_t[:], ACT.Abs_reciprocal_sqrt, bias=TINY)
        nc.scalar.activation(sign[:], gs_t[:], ACT.Sign)
        nc.scalar.activation(half_inv[:], inv_root[:], ACT.Copy, scale=-0.5)
        nc.scalar.activation(h_scale[:], sign[:], ACT.Copy, scale=-0.0625)
        for c in cells:
            nc.scalar.activation(guess[:, c], gs_t[:, c], ACT.Abs, scale=inv_root[:, c])
        for c in cells:
            nc.scalar.activation(mend[:, c], guess[:, c], ACT.Identity, scale=half_inv[:, c], bias=1.5)
        for c in cells:
            nc.scalar.activation(root[:, c], guess[:, c], ACT.Copy, scale=mend[:, c])

        def pick_scales(i, codes, tag):
            picked = sb("picked_bytes%d" % i, [P, H], U8, tag=tag)
            nc.vector.tensor_copy(picked[:], d_bytes[:].indirect(codes[:]))
            return picked

        def deal_scales(i, picked, queue):
            dealt = sb("dealt_bytes%d" % i, [P, H], U8)
            nc.vector.tensor_copy(
                dealt[:].rearrange("p (t m) -> p m t", t=PACK), picked[:].rearrange("p (m t) -> p m t", t=PACK)
            )
            for q in range(4):
                queue.dma_start(
                    w_plane[i][32 * q : 32 * q + 4, :].bitcast(I32), dealt[32 * q : 32 * q + 32 : 8, :].bitcast(I32)
                )

        def pick_words(name, codes, tag):
            picked = sb(name, [P, 16 * codes.shape[1]], U32, tag=tag)
            nc.vector.tensor_copy(picked[:], d_codes[:].bitcast(U32).indirect(codes))
            return picked

        def deal_words(dealt, picked, m0):
            m1 = m0 + picked.shape[1] // PACK
            nc.vector.tensor_copy(
                dealt[:].bitcast(I32).rearrange("p (t m) -> p m t", t=PACK)[:, m0:m1, :],
                picked[:].bitcast(I32).rearrange("p (m t) -> p m t", t=PACK),
            )

        w1 = sb("w1", [P, H], U32)
        w2 = sb("w2", [P, H], U32)
        xq_words = sb("xq_words", [P, S], U32)
        xq_plane = sb("xq_plane", [P, S], U8)
        bytes1 = pick_scales(0, k1_t, "")
        nc.vector.tensor_copy(xq_plane[:], x_bytes[:].indirect(offs_t[:]))
        deal_scales(0, bytes1, nc.scalar)
        nc.vector.tensor_copy(xq_words[:], x_codes[:].bitcast(U32).indirect(offs_t[:]))
        words1 = [pick_words("words1_%d" % u, k1_t[:, 16 * u : 16 * (u + 1)], "early%d" % u) for u in range(2)]
        for u in range(2):
            deal_words(w1, words1[u], P // 2 * u)
        bytes2 = pick_scales(1, k2_t, "early0")
        words2 = pick_words("words2", k2_t[:], "early1")

        def product(out, i, words, t, rhs_words, rhs_plane, cols):
            rows = slice(P * t, P * (t + 1))
            nc.tensor.matmul_mx(
                out=out,
                lhsT=words[:, rows].bitcast(FP8X4),
                lhsT_scale=w_plane[i][:, rows],
                rhs=rhs_words[:, cols].bitcast(FP8X4),
                rhs_scale=rhs_plane[:, cols],
                start=True,
                stop=True,
            )

        h_bank = [psum.tile([P, S], F32, name="h_bank%d" % t, tag="bank%d" % t) for t in range(PACK)]
        for t in (0, 2, 1, 3):
            product(h_bank[t][:], 0, w1, t, xq_words, xq_plane, slice(0, S))

        deal_scales(1, bytes2, nc.sync)

        st = sb("st", [P, PACK, S], F32)
        mag = sb("mag", [P, PACK, S], F32)
        gain = [sb("gain%d" % t, [P, 2 * S], F32) for t in range(PACK)]
        z = sb("z", [P, PACK, S], F32)

        def spill(t):
            nc.scalar.activation(h_win[t][:, :S], h_bank[t][:], ACT.Copy, scale=h_scale[:, t : t + 1])
            if t < 2:
                nc.scalar.activation(h_own[t], h_bank[t][:], ACT.Copy, scale=h_scale[:, t : t + 1])
            else:
                nc.sync.dma_start(h_own[t], h_win[t][:, :S])

        def step(t):
            nc.vector.tensor_tensor(st[:, t, :], h_win[t][:].indirect(n1_t[:]), h_own[t], ALU.subtract)

        def weigh(t):
            for a in (0, HALF):
                nc.scalar.activation(mag[:, t, a : a + HALF], st[:, t, a : a + HALF], ACT.Abs)
            for a in (0, HALF):
                nc.scalar.activation(
                    gain[t][:, S + a : S + a + HALF], mag[:, t, a : a + HALF], ACT.Abs_reciprocal_sqrt, bias=0.5
                )
            for a in (0, HALF):
                nc.scalar.activation(
                    gain[t][:, a : a + HALF], gain[t][:, S + a : S + a + HALF], ACT.Square, scale=root[:, t : t + 1]
                )

        def divide(t, a, b):
            places = n2_t[:, a // 16 : b // 16]
            nc.vector.tensor_tensor(z[:, t, a:b], gain[t][:].indirect(places), st[:, t, a:b], ALU.mult)

        z_packed = sb("z_packed", [P, S * PACK], BF16)
        z_words = sb("z_words", [P, S], U32)
        z_plane = sb("z_plane", [P, S], U8)

        def weave(copy, a, b):
            copy(
                z_packed[:, PACK * a : PACK * b].rearrange("p (c i t) -> p c t i", i=4, t=PACK),
                z[:, :, a:b].rearrange("p t (c i) -> p c t i", i=4),
            )

        for t in (0, 2, 1, 3):
            spill(t)
        step(0)
        deal_words(w2, words2, 0)
        step(1)
        for t in range(2, PACK):
            step(t)
        for t in range(PACK):
            weigh(t)
        for t in range(PACK - 1):
            divide(t, 0, S)
        quarter = S // 4
        for a in range(0, S, quarter):
            divide(3, a, a + quarter)
            weave(nc.vector.tensor_copy if a + quarter == S else nc.scalar.copy, a, a + quarter)

        h2_bank = [
            [psum.tile([P, HALF], F32, name="h2_bank%d_%d" % (u, t), tag="bank%d" % (PACK * (1 - u) + t)) for t in range(PACK)]
            for u in range(2)
        ]
        halves = [slice(HALF * u, HALF * (u + 1)) for u in range(2)]
        for u in range(2):
            wide = slice(PACK * HALF * u, PACK * HALF * (u + 1))
            nc.vector.quantize_mx(
                out=z_words[:, halves[u]].bitcast(FP8X4), scales=z_plane[:, halves[u]], in_=z_packed[:, wide]
            )
        for t in range(PACK):
            for u in range(2):
                product(h2_bank[u][t][:], 1, w2, t, z_words, z_plane, halves[u])

        res = [sb("res%d" % t, [P, S], F32) for t in range(PACK)]
        pa = sb("pa", [P, PACK, W], F32)
        pb = sb("pb", [P, PACK, W], F32)
        sa = sb("sa", [P, PACK, W], F32)
        sbb = sb("sbb", [P, PACK, W], F32)
        y_packed = sb("y_packed", [P, S, PACK], BF16)
        y_words = sb("y_words", [P, S], U32)
        y_plane = sb("y_plane", [P, S], U8)
        out_rows = out_0.rearrange("(p t) s -> t p s", t=PACK)

        h2 = [sb("h2_%d" % t, [P, S], F32) for t in range(PACK)]
        gap = sb("gap", [P, PACK, W], F32)
        turned = sb("turned", [P, PACK, W], F32)

        def fetch(t):
            for u in range(2):
                nc.scalar.activation(h2[t][:, halves[u]], h2_bank[u][t][:], ACT.Copy, scale=0.0625)
            nc.vector.tensor_copy(pa[:, t, :], h2[t][:].indirect(n3_t[:]))

        def face(t):
            nc.vector.tensor_tensor(gap[:, t, :], h2[t][:].indirect(n4_t[:]), pa[:, t, :], ALU.subtract)

        def gate_a(t):
            nc.scalar.activation(sa[:, t, :], gap[:, t, :], ACT.Sigmoid, scale=-1.0)

        def gate_b(t):
            there = psum.tile([P, W], F32, name="there%d" % t, tag="bank%d" % t)
            back = psum.tile([P, W], F32, name="back%d" % t, tag="bank%d" % (PACK + t))
            for c in range(0, W, P):
                for first, part in ((True, pa), (False, gap)):
                    nc.tensor.matmul(
                        there[:, c : c + P], part[:, t, c : c + P], ident[:], start=first, stop=not first, is_transpose=True
                    )
            nc.scalar.copy(turned[:, t, :], there[:])
            for c in range(0, W, P):
                nc.tensor.transpose(back[:, c : c + P], turned[:, t, c : c + P], ident[:])
            nc.scalar.activation(sbb[:, t, :], gap[:, t, :], ACT.Sigmoid)
            nc.scalar.copy(pb[:, t, :], back[:])

        def put_a(t):
            nc.vector.tensor_tensor(res[t][:].indirect(n3_t[:]), pa[:, t, :], sa[:, t, :], ALU.mult)

        def put_b(t):
            nc.vector.tensor_tensor(res[t][:].indirect(n4_t[:]), pb[:, t, :], sbb[:, t, :], ALU.mult)
            nc.sync.dma_start(out_rows[t], res[t][:])

        split = 3 * quarter
        fetch(0)
        for t in range(1, PACK):
            fetch(t)
            face(t - 1)
        face(PACK - 1)
        gate_a(0)
        for t in range(1, PACK):
            gate_a(t)
            gate_b(t - 1)
        gate_b(PACK - 1)
        put_a(0)
        for t in range(2):
            put_a(t + 1)
            put_b(t)
            nc.scalar.copy(y_packed[:, :, t], res[t][:])
        put_a(3)
        put_b(2)
        nc.scalar.copy(y_packed[:, :split, 2:], res[2][:, :split].unsqueeze(2).to_broadcast([P, split, 2]))
        nc.scalar.copy(y_packed[:, split:, 2], res[2][:, split:])
        put_b(3)
        nc.scalar.copy(y_packed[:, split:, 3], res[3][:, split:])
        nc.vector.tensor_copy(y_packed[:, :HALF, 3], res[3][:, :HALF])
        nc.vector.tensor_copy(y_packed[:, HALF:split, 3], res[3][:, HALF:split])

        words_out = out_1[0].rearrange("p n t -> p (n t)").bitcast(I32)
        for u in range(2):
            nc.vector.quantize_mx(
                out=y_words[:, halves[u]].bitcast(FP8X4),
                scales=y_plane[:, halves[u]],
                in_=y_packed[:, halves[u], :].rearrange("p s t -> p (s t)"),
            )
            nc.sync.dma_start(words_out[:, halves[u]], y_words[:, halves[u]].bitcast(I32))
        for q in range(4):
            (nc.scalar if q < 2 else nc.sync).dma_start(
                out_2[0, 4 * q : 4 * q + 4, :].bitcast(I32), y_plane[32 * q : 32 * q + 4, :].bitcast(I32)
            )
